import numpy as np, ml_dtypes
CORES = [21,109,149,237,277,365,405,493,150,406]
N = 10
S, B = 2, 512
def setup_inputs(rng):
    a = (rng.standard_normal((128, 128), dtype=np.float32) / 8).astype(ml_dtypes.bfloat16)
    return {"x": (rng.standard_normal((N, 128, S * B), dtype=np.float32) / 2).astype(ml_dtypes.bfloat16), "a": np.broadcast_to(a, (N, 128, 128)).copy()}
def reference(x, a):
    X, A = x.astype(np.float64), a.astype(np.float64)
    y = np.zeros((N, 128, S * B)); h = np.zeros((128, B))
    for r in range(N):
        for s in range(S):
            h = np.tanh(A[r].T @ h + X[r][:, B * s:B * s + B])
            y[r][:, B * s:B * s + B] = h
    return {"y": y.astype(ml_dtypes.bfloat16)}

@@ -1,0 +1,235 @@
+import comms_topo
+from concourse.bass import DstId, RemoteDMATransfer
+from concourse.mybir import AluOpType, ActivationFunctionType
+
+N, S, B, P = 10, 2, 512, 128
+NCORES = 512
+W = 8
+w = B // W
+PW = S * w
+
+GROUPS = [[0, 2], [1, 3], [4, 6], [5, 7], [8], [9]]
+HOME = [0, 1, 2, 3, 3, 3]
+ANCHOR = [2, 3, 4, 5]
+SERVE = [[0, 1, 2], [3, 4, 5], [6, 7], [8, 9]]
+A_GROUP, A_RANK = 0, 8
+
+GROUP_OF, XOFF, GOFF, GSIZE = {}, {}, [], []
+_o = 0
+for _g, _rs in enumerate(GROUPS):
+    GOFF.append(_o)
+    for _r in _rs:
+        GROUP_OF[_r] = _g
+        XOFF[_r] = _o
+        _o += PW
+    if _g == A_GROUP:
+        AOFF = _o
+        _o += P
+    GSIZE.append(_o - GOFF[_g])
+XL = _o
+NEED = [[_g for _g, _rs in enumerate(GROUPS) if min(_rs) <= max(SERVE[_f])] for _f in range(4)]
+
+SCRATCH = {
+    "xin": ("sbuf", [P, S, W, w], "bfloat16"),
+    "stg": ("sbuf", [P, W, PW], "bfloat16"),
+    "ain": ("sbuf", [P, P], "bfloat16"),
+    "yl": ("sbuf", [P, W, PW], "bfloat16"),
+    "yo": ("sbuf", [P, S, W, w], "bfloat16"),
+    "xl": ("sbuf", [P, XL], "bfloat16"),
+    "hb": ("sbuf", [P, N * PW], "bfloat16"),
+    "ones": ("sbuf", [P, P], "bfloat16"),
+    "ident": ("sbuf", [P, P], "bfloat16"),
+    "ps0": ("psum", [P, 512], "float32"),
+    "ps1": ("psum", [P, 512], "float32"),
+}
+SEMAPHORES = ["ld0", "ld1", "lda", "shuf", "sent", "sy", "un0", "un1", "st",
+              "g0", "g1", "g2", "g3", "g4", "g5", "ms", "idn", "mm", "act"]
+
+_CACHE = {}
+
+
+def _engines(topo, src, dsts):
+    m = topo.mask(src, dsts[0])
+    for d in dsts:
+        m &= topo.mask(src, d)
+    return [1 << b for b in range(16) if (m >> b) & 1]
+
+
+def _join(bits):
+    m = 0
+    for b in bits:
+        m |= b
+    return m
+
+
+def _dst(topo, d, src):
+    rid, pid = topo.addr(d, src)
+    return DstId(rid=rid, pnc=pid)
+
+
+def _plan(T, topo):
+    if "p" in _CACHE:
+        return _CACHE["p"]
+    C = list(T.cores)
+    fam = []
+    for f, ar in enumerate(ANCHOR):
+        a = C[ar]
+        must = [C[r] for r in ANCHOR] + [C[r] for r in SERVE[f]]
+        bychip = {}
+        for c in range(NCORES):
+            if topo.host(c) != topo.host(a) or c in C:
+                continue
+            if not topo.may_write(a, c) or topo.die(c) != topo.die(a):
+                continue
+            if all(topo.may_write(c, d) for d in must):
+                bychip.setdefault(topo.chip(c), c)
+        fam.append(bychip)
+
+    def busy(c):
+        return any(topo.host(d) == topo.host(c) and topo.chip(d) == topo.chip(c) for d in C)
+
+    cols = []
+    for ch in sorted(fam[0]):
+        c0, c2 = fam[0][ch], fam[2][ch]
+        c1 = [c for c in fam[1].values() if topo.mates(c0, c)][0]
+        c3 = [c for c in fam[3].values() if topo.mates(c2, c)][0]
+        cols.append([c0, c1, c2, c3])
+    cols.sort(key=lambda q: any(busy(c) for c in q))
+    cols = cols[:W]
+    where = {}
+    for j, q in enumerate(cols):
+        for f, c in enumerate(q):
+            where[c] = (f, j)
+    _CACHE["p"] = {"cols": cols, "where": where}
+    return _CACHE["p"]
+
+
+def _scatter_engines(topo, C, pl, r):
+    sites = [pl["cols"][j][HOME[GROUP_OF[r]]] for j in range(W)]
+    bits = _engines(topo, C[r], sites)
+    per = len(bits) // W
+    return sites, [bits[j * per:(j + 1) * per] for j in range(W)]
+
+
+def _threshold(topo, C, pl, f, j, grp):
+    if HOME[grp] != f:
+        src = pl["cols"][j][HOME[grp]]
+        return len(_engines(topo, src, _targets(pl, j, grp)))
+    n = sum(len(_scatter_engines(topo, C, pl, r)[1][j]) for r in GROUPS[grp])
+    if grp == A_GROUP:
+        n += len(_engines(topo, C[A_RANK], [pl["cols"][k][f] for k in range(W)]))
+    return n
+
+
+def _targets(pl, j, grp):
+    return [pl["cols"][j][f] for f in (3, 2, 1, 0) if f != HOME[grp] and grp in NEED[f]]
+
+
+def _rank(g, core, r, T, topo, pl):
+    sem, C, v = T.sem, list(T.cores), g.vector
+    sent = 0
+    if r == A_RANK:
+        g.sync.dma_start(T.ain[:], T.a[:]).then_inc(sem.lda, 16)
+    g.sync.dma_start(T.xin[:, 0], T.x[:, 0:B]).then_inc(sem.ld0, 16)
+    g.scalar.dma_start(T.xin[:, 1], T.x[:, B:2 * B]).then_inc(sem.ld1, 16)
+    v.wait_ge(sem.ld0, 16)
+    v.tensor_copy(T.stg[:, :, 0:w], T.xin[:, 0]).then_inc(sem.shuf, 1)
+    v.wait_ge(sem.ld1, 16)
+    v.tensor_copy(T.stg[:, :, w:2 * w], T.xin[:, 1]).then_inc(sem.shuf, 1)
+    if r == A_RANK:
+        asites = [pl["cols"][k][HOME[A_GROUP]] for k in range(W)]
+        bits = _engines(topo, core, asites)
+        g.wait_ge(sem.lda, 16)
+        g.remote_dma_fused([RemoteDMATransfer(
+            dst_ids=[_dst(topo, d, core) for d in asites], dma_engine_mask=_join(bits),
+            remote_sem=sem["g%d" % A_GROUP], srcs=[T.ain[:]],
+            dsts=[T.xl[:, AOFF:AOFF + P] for d in asites])], local_sem=sem.sent)
+        sent += len(bits)
+    sites, eng = _scatter_engines(topo, C, pl, r)
+    g.wait_ge(sem.shuf, 2)
+    g.remote_dma_fused([RemoteDMATransfer(
+        dst_ids=[_dst(topo, sites[j], core)], dma_engine_mask=_join(eng[j]), remote_sem=sem["g%d" % GROUP_OF[r]],
+        src=T.stg[:, j, :], dst=T.xl[:, XOFF[r]:XOFF[r] + PW]) for j in range(W)], local_sem=sem.sent)
+    sent += sum(len(e) for e in eng)
+    f = [k for k in range(4) if r in SERVE[k]][0]
+    total = sum(len(_engines(topo, pl["cols"][j][f], [core])) for j in range(W))
+    v.wait_ge(sem.sy, total)
+    v.tensor_copy(T.yo[:, 0], T.yl[:, :, 0:w]).then_inc(sem.un0, 1)
+    v.tensor_copy(T.yo[:, 1], T.yl[:, :, w:2 * w]).then_inc(sem.un1, 1)
+    g.sync.wait_ge(sem.un0, 1)
+    g.sync.dma_start(T.y[:, 0:B], T.yo[:, 0]).then_inc(sem.st, 16)
+    g.scalar.wait_ge(sem.un1, 1)
+    g.scalar.dma_start(T.y[:, B:2 * B], T.yo[:, 1]).then_inc(sem.st, 16)
+    g.wait_ge(sem.sent, sent)
+    g.wait_ge(sem.st, 32)
+
+
+def _site(g, core, f, j, T, topo, pl):
+    sem, C = T.sem, list(T.cores)
+    pe, act = g.tensor, g.scalar
+    nt = S * (max(SERVE[f]) + 1)
+    thr = {grp: _threshold(topo, C, pl, f, j, grp) for grp in NEED[f]}
+    ps = [T.ps0, T.ps1]
+
+    def x_of(t):
+        o = XOFF[t // S] + (t % S) * w
+        return T.xl[:, o:o + w]
+
+    def h_of(t):
+        return T.hb[:, t * w:(t + 1) * w]
+
+    g.vector.memset(T.ones[:], 1.0).then_inc(sem.ms, 1)
+    g.wait_ge(sem.ms, 1)
+    g.affine_select(T.ident[:], T.ones[:], [[-1, P]], AluOpType.is_equal, 0.0, 0, 1).then_inc(sem.idn, 1)
+    sent = 0
+    for grp in NEED[f]:
+        tg = _targets(pl, j, grp)
+        if HOME[grp] != f or not tg:
+            continue
+        bits = _engines(topo, core, tg)
+        piece = T.xl[:, GOFF[grp]:GOFF[grp] + GSIZE[grp]]
+        g.wait_ge(sem["g%d" % grp], thr[grp])
+        g.remote_dma_fused([RemoteDMATransfer(
+            dst_ids=[_dst(topo, d, core) for d in tg], dma_engine_mask=_join(bits), remote_sem=sem["g%d" % grp],
+            srcs=[piece], dsts=[piece for d in tg])], local_sem=sem.sent)
+        sent += len(bits)
+    for r in SERVE[f]:
+        bits = _engines(topo, core, [C[r]])
+        rid, pid = topo.addr(C[r], core)
+        g.wait_ge(sem.act, S * r + S)
+        g.remote_dma(T.yl[:, j, :], T.hb[:, r * PW:(r + 1) * PW], sem.sy, sem.sent, pid, rid, _join(bits))
+        sent += len(bits)
+    g.wait_ge(sem.sent, sent)
+
+    seen = set()
+
+    def pre(t):
+        grp = GROUP_OF[t // S]
+        if grp not in seen:
+            seen.add(grp)
+            pe.wait_ge(sem["g%d" % grp], thr[grp])
+        pe.matmul(ps[t % 2][:, 0:w], T.ident[:], x_of(t), True, False)
+
+    pe.wait_ge(sem.idn, 1)
+    pre(1)
+    for t in range(1, nt):
+        pe.wait_ge(sem.act, t)
+        pe.matmul(ps[t % 2][:, 0:w], T.xl[:, AOFF:AOFF + P], h_of(t - 1), False, True).then_inc(sem.mm, 1)
+        if t + 1 < nt:
+            pre(t + 1)
+
+    act.wait_ge(sem["g%d" % GROUP_OF[0]], thr[GROUP_OF[0]])
+    act.activation(h_of(0), x_of(0), ActivationFunctionType.Tanh).then_inc(sem.act, 1)
+    for t in range(1, nt):
+        act.wait_ge(sem.mm, t)
+        act.activation(h_of(t), ps[t % 2][:, 0:w], ActivationFunctionType.Tanh).then_inc(sem.act, 1)
+
+
+def rank_program(g, core, T, topo):
+    pl = _plan(T, topo)
+    r = T.rank_of(core)
+    if r is not None:
+        _rank(g, core, r, T, topo, pl)
+    elif core in pl["where"]:
+        f, j = pl["where"][core]
+        _site(g, core, f, j, T, topo, pl)

@@ -9,10 +9,15 @@ w = B // W
 PW = S * w
 
 GROUPS = [[0, 2], [1, 3], [4, 6], [5, 7], [8], [9]]
-HOME = [0, 1, 2, 3, 3, 3]
+HOME = [0, 1, 2, 3, 4, 3]
+FWD = [1, 0, 3, 2, 3, None]
 ANCHOR = [2, 3, 4, 5]
-SERVE = [[0, 1, 2], [3, 4, 5], [6, 7], [8, 9]]
-A_GROUP, A_RANK = 0, 8
+SERVE = [[0, 1], [2, 3], [4, 5, 6], [7, 8, 9]]
+NEED = [[0, 1], [0, 1], [2, 3], [2, 3, 4, 5]]
+T0 = [0, 0, 8, 8]
+NEXT = [2, 3, None, None]
+A_GROUP, A_RANK = 1, 8
+BACK_RANK, BACK_FAM = 8, 1
 
 GROUP_OF, XOFF, GOFF, GSIZE = {}, {}, [], []
 _o = 0
@@ -27,7 +32,6 @@ for _g, _rs in enumerate(GROUPS):
         _o += P
     GSIZE.append(_o - GOFF[_g])
 XL = _o
-NEED = [[_g for _g, _rs in enumerate(GROUPS) if min(_rs) <= max(SERVE[_f])] for _f in range(4)]
 
 SCRATCH = {
     "xin": ("sbuf", [P, S, W, w], "bfloat16"),
@@ -43,7 +47,7 @@ SCRATCH = {
     "ps1": ("psum", [P, 512], "float32"),
 }
 SEMAPHORES = ["ld0", "ld1", "lda", "shuf", "sent", "sy", "un0", "un1", "st",
-              "g0", "g1", "g2", "g3", "g4", "g5", "ms", "idn", "mm", "act"]
+              "g0", "g1", "g2", "g3", "g4", "g5", "ga", "hh", "yr", "ms", "idn", "mm", "act"]
 
 _CACHE = {}
 
@@ -74,7 +78,9 @@ def _plan(T, topo):
     fam = []
     for f, ar in enumerate(ANCHOR):
         a = C[ar]
-        must = [C[r] for r in ANCHOR] + [C[r] for r in SERVE[f]]
+        must = [C[r] for r in ANCHOR] + [C[r] for r in SERVE[f] if r != BACK_RANK]
+        if f == BACK_FAM:
+            must.append(C[BACK_RANK])
         bychip = {}
         for c in range(NCORES):
             if topo.host(c) != topo.host(a) or c in C:
@@ -84,17 +90,14 @@ def _plan(T, topo):
             if all(topo.may_write(c, d) for d in must):
                 bychip.setdefault(topo.chip(c), c)
         fam.append(bychip)
-
-    def busy(c):
-        return any(topo.host(d) == topo.host(c) and topo.chip(d) == topo.chip(c) for d in C)
-
     cols = []
     for ch in sorted(fam[0]):
         c0, c2 = fam[0][ch], fam[2][ch]
         c1 = [c for c in fam[1].values() if topo.mates(c0, c)][0]
         c3 = [c for c in fam[3].values() if topo.mates(c2, c)][0]
-        cols.append([c0, c1, c2, c3])
-    cols.sort(key=lambda q: any(busy(c) for c in q))
+        k = [c for c in range(NCORES) if topo.host(c) == topo.host(c1) and topo.chip(c) == topo.chip(c1)
+             and topo.die(c) == topo.die(c1) and c not in C and not topo.may_write(c, c0) and topo.may_write(c, c3)][0]
+        cols.append([c0, c1, c2, c3, k])
     cols = cols[:W]
     where = {}
     for j, q in enumerate(cols):
@@ -113,16 +116,18 @@ def _scatter_engines(topo, C, pl, r):
 
 def _threshold(topo, C, pl, f, j, grp):
     if HOME[grp] != f:
-        src = pl["cols"][j][HOME[grp]]
-        return len(_engines(topo, src, _targets(pl, j, grp)))
+        return len(_engines(topo, pl["cols"][j][HOME[grp]], [pl["cols"][j][f]]))
     n = sum(len(_scatter_engines(topo, C, pl, r)[1][j]) for r in GROUPS[grp])
     if grp == A_GROUP:
         n += len(_engines(topo, C[A_RANK], [pl["cols"][k][f] for k in range(W)]))
     return n
 
 
-def _targets(pl, j, grp):
-    return [pl["cols"][j][f] for f in (3, 2, 1, 0) if f != HOME[grp] and grp in NEED[f]]
+def _send(g, topo, core, d, out, in_, rsem, lsem):
+    bits = _engines(topo, core, [d])
+    rid, pid = topo.addr(d, core)
+    g.remote_dma(out, in_, rsem, lsem, pid, rid, _join(bits))
+    return len(bits)
 
 
 def _rank(g, core, r, T, topo, pl):
@@ -151,7 +156,7 @@ def _rank(g, core, r, T, topo, pl):
         dst_ids=[_dst(topo, sites[j], core)], dma_engine_mask=_join(eng[j]), remote_sem=sem["g%d" % GROUP_OF[r]],
         src=T.stg[:, j, :], dst=T.xl[:, XOFF[r]:XOFF[r] + PW]) for j in range(W)], local_sem=sem.sent)
     sent += sum(len(e) for e in eng)
-    f = [k for k in range(4) if r in SERVE[k]][0]
+    f = BACK_FAM if r == BACK_RANK else [k for k in range(4) if r in SERVE[k]][0]
     total = sum(len(_engines(topo, pl["cols"][j][f], [core])) for j in range(W))
     v.wait_ge(sem.sy, total)
     v.tensor_copy(T.yo[:, 0], T.yl[:, :, 0:w]).then_inc(sem.un0, 1)
@@ -164,12 +169,25 @@ def _rank(g, core, r, T, topo, pl):
     g.wait_ge(sem.st, 32)
 
 
-def _site(g, core, f, j, T, topo, pl):
+def _relay(g, core, j, T, topo, pl):
     sem, C = T.sem, list(T.cores)
+    grp = GROUP_OF[A_RANK]
+    piece = T.xl[:, GOFF[grp]:GOFF[grp] + GSIZE[grp]]
+    g.wait_ge(sem["g%d" % grp], _threshold(topo, C, pl, 4, j, grp))
+    n = _send(g, topo, core, pl["cols"][j][FWD[grp]], piece, piece, sem["g%d" % grp], sem.sent)
+    g.wait_ge(sem.sent, n)
+
+
+def _site(g, core, f, j, T, topo, pl):
+    sem, C, col = T.sem, list(T.cores), pl["cols"][j]
     pe, act = g.tensor, g.scalar
-    nt = S * (max(SERVE[f]) + 1)
+    t0 = T0[f]
+    nt = T0[NEXT[f]] if NEXT[f] is not None else S * (max(SERVE[f]) + 1)
     thr = {grp: _threshold(topo, C, pl, f, j, grp) for grp in NEED[f]}
     ps = [T.ps0, T.ps1]
+    a_ap = T.xl[:, AOFF:AOFF + P]
+    prev = [k for k in range(4) if NEXT[k] == f]
+    n_in = len(_engines(topo, col[prev[0]], [core])) if prev else 0
 
     def x_of(t):
         o = XOFF[t // S] + (t % S) * w
@@ -178,50 +196,68 @@ def _site(g, core, f, j, T, topo, pl):
     def h_of(t):
         return T.hb[:, t * w:(t + 1) * w]
 
+    def y_of(r):
+        return T.hb[:, r * PW:(r + 1) * PW]
+
     g.vector.memset(T.ones[:], 1.0).then_inc(sem.ms, 1)
     g.wait_ge(sem.ms, 1)
     g.affine_select(T.ident[:], T.ones[:], [[-1, P]], AluOpType.is_equal, 0.0, 0, 1).then_inc(sem.idn, 1)
     sent = 0
     for grp in NEED[f]:
-        tg = _targets(pl, j, grp)
-        if HOME[grp] != f or not tg:
-            continue
-        bits = _engines(topo, core, tg)
-        piece = T.xl[:, GOFF[grp]:GOFF[grp] + GSIZE[grp]]
-        g.wait_ge(sem["g%d" % grp], thr[grp])
-        g.remote_dma_fused([RemoteDMATransfer(
-            dst_ids=[_dst(topo, d, core) for d in tg], dma_engine_mask=_join(bits), remote_sem=sem["g%d" % grp],
-            srcs=[piece], dsts=[piece for d in tg])], local_sem=sem.sent)
-        sent += len(bits)
+        if HOME[grp] == f and FWD[grp] is not None:
+            piece = T.xl[:, GOFF[grp]:GOFF[grp] + GSIZE[grp]]
+            g.wait_ge(sem["g%d" % grp], thr[grp])
+            sent += _send(g, topo, core, col[FWD[grp]], piece, piece, sem["g%d" % grp], sem.sent)
+    if NEXT[f] is not None:
+        g.wait_ge(sem["g%d" % A_GROUP], thr[A_GROUP])
+        sent += _send(g, topo, core, col[NEXT[f]], a_ap, a_ap, sem.ga, sem.sent)
+        g.wait_ge(sem.act, nt - t0)
+        sent += _send(g, topo, core, col[NEXT[f]], h_of(nt - 1), h_of(nt - 1), sem.hh, sem.sent)
     for r in SERVE[f]:
-        bits = _engines(topo, core, [C[r]])
-        rid, pid = topo.addr(C[r], core)
-        g.wait_ge(sem.act, S * r + S)
-        g.remote_dma(T.yl[:, j, :], T.hb[:, r * PW:(r + 1) * PW], sem.sy, sem.sent, pid, rid, _join(bits))
-        sent += len(bits)
+        g.wait_ge(sem.act, S * r + S - t0)
+        if r == BACK_RANK:
+            sent += _send(g, topo, core, col[BACK_FAM], y_of(r), y_of(r), sem.yr, sem.sent)
+        else:
+            sent += _send(g, topo, core, C[r], T.yl[:, j, :], y_of(r), sem.sy, sem.sent)
+    if f == BACK_FAM:
+        src = col[[k for k in range(4) if BACK_RANK in SERVE[k]][0]]
+        g.wait_ge(sem.yr, len(_engines(topo, src, [core])))
+        sent += _send(g, topo, core, C[BACK_RANK], T.yl[:, j, :], y_of(BACK_RANK), sem.sy, sem.sent)
     g.wait_ge(sem.sent, sent)
 
     seen = set()
 
-    def pre(t):
-        grp = GROUP_OF[t // S]
+    def need(grp):
         if grp not in seen:
             seen.add(grp)
             pe.wait_ge(sem["g%d" % grp], thr[grp])
+
+    def pre(t):
+        need(GROUP_OF[t // S])
         pe.matmul(ps[t % 2][:, 0:w], T.ident[:], x_of(t), True, False)
 
+    first = t0 if prev else t0 + 1
     pe.wait_ge(sem.idn, 1)
-    pre(1)
-    for t in range(1, nt):
-        pe.wait_ge(sem.act, t)
-        pe.matmul(ps[t % 2][:, 0:w], T.xl[:, AOFF:AOFF + P], h_of(t - 1), False, True).then_inc(sem.mm, 1)
+    pre(first)
+    for t in range(first, nt):
+        if t == first:
+            if prev:
+                pe.wait_ge(sem.ga, n_in)
+            else:
+                need(A_GROUP)
+        if t == t0:
+            pe.wait_ge(sem.hh, n_in)
+        else:
+            pe.wait_ge(sem.act, t - t0)
+        pe.matmul(ps[t % 2][:, 0:w], a_ap, h_of(t - 1), False, True).then_inc(sem.mm, 1)
         if t + 1 < nt:
             pre(t + 1)
 
-    act.wait_ge(sem["g%d" % GROUP_OF[0]], thr[GROUP_OF[0]])
-    act.activation(h_of(0), x_of(0), ActivationFunctionType.Tanh).then_inc(sem.act, 1)
-    for t in range(1, nt):
-        act.wait_ge(sem.mm, t)
+    if not prev:
+        act.wait_ge(sem["g%d" % GROUP_OF[0]], thr[GROUP_OF[0]])
+        act.activation(h_of(0), x_of(0), ActivationFunctionType.Tanh).then_inc(sem.act, 1)
+    for t in range(first, nt):
+        act.wait_ge(sem.mm, t - first + 1)
         act.activation(h_of(t), ps[t % 2][:, 0:w], ActivationFunctionType.Tanh).then_inc(sem.act, 1)
 
 
@@ -232,4 +268,7 @@ def rank_program(g, core, T, topo):
         _rank(g, core, r, T, topo, pl)
     elif core in pl["where"]:
         f, j = pl["where"][core]
-        _site(g, core, f, j, T, topo, pl)
+        if f == 4:
+            _relay(g, core, j, T, topo, pl)
+        else:
+            _site(g, core, f, j, T, topo, pl)

import comms_topo
from concourse.bass import DstId, RemoteDMATransfer
from concourse.mybir import AluOpType, ActivationFunctionType

N, S, B, P = 10, 2, 512, 128
NCORES = 512
W = 8
w = B // W
PW = S * w

GROUPS = [[0, 2], [1, 3], [4, 6], [5, 7], [8], [9]]
HOME = [0, 1, 2, 3, 4, 3]
FWD = [1, 0, 3, 2, 3, None]
ANCHOR = [2, 3, 4, 5]
SERVE = [[0, 1], [2, 3], [4, 5, 6], [7, 8, 9]]
NEED = [[0, 1], [0, 1], [2, 3], [2, 3, 4, 5]]
T0 = [0, 0, 8, 8]
NEXT = [2, 3, None, None]
A_GROUP, A_RANK = 1, 8
BACK_RANK, BACK_FAM = 8, 1

GROUP_OF, XOFF, GOFF, GSIZE = {}, {}, [], []
_o = 0
for _g, _rs in enumerate(GROUPS):
    GOFF.append(_o)
    for _r in _rs:
        GROUP_OF[_r] = _g
        XOFF[_r] = _o
        _o += PW
    if _g == A_GROUP:
        AOFF = _o
        _o += P
    GSIZE.append(_o - GOFF[_g])
XL = _o

SCRATCH = {
    "xin": ("sbuf", [P, S, W, w], "bfloat16"),
    "stg": ("sbuf", [P, W, PW], "bfloat16"),
    "ain": ("sbuf", [P, P], "bfloat16"),
    "yl": ("sbuf", [P, W, PW], "bfloat16"),
    "yo": ("sbuf", [P, S, W, w], "bfloat16"),
    "xl": ("sbuf", [P, XL], "bfloat16"),
    "hb": ("sbuf", [P, N * PW], "bfloat16"),
    "ones": ("sbuf", [P, P], "bfloat16"),
    "ident": ("sbuf", [P, P], "bfloat16"),
    "ps0": ("psum", [P, 512], "float32"),
    "ps1": ("psum", [P, 512], "float32"),
}
SEMAPHORES = ["ld0", "ld1", "lda", "shuf", "sent", "sy", "un0", "un1", "st",
              "g0", "g1", "g2", "g3", "g4", "g5", "ga", "hh", "yr", "ms", "idn", "mm", "act"]

_CACHE = {}


def _engines(topo, src, dsts):
    m = topo.mask(src, dsts[0])
    for d in dsts:
        m &= topo.mask(src, d)
    return [1 << b for b in range(16) if (m >> b) & 1]


def _join(bits):
    m = 0
    for b in bits:
        m |= b
    return m


def _dst(topo, d, src):
    rid, pid = topo.addr(d, src)
    return DstId(rid=rid, pnc=pid)


def _plan(T, topo):
    if "p" in _CACHE:
        return _CACHE["p"]
    C = list(T.cores)
    fam = []
    for f, ar in enumerate(ANCHOR):
        a = C[ar]
        must = [C[r] for r in ANCHOR] + [C[r] for r in SERVE[f] if r != BACK_RANK]
        if f == BACK_FAM:
            must.append(C[BACK_RANK])
        bychip = {}
        for c in range(NCORES):
            if topo.host(c) != topo.host(a) or c in C:
                continue
            if not topo.may_write(a, c) or topo.die(c) != topo.die(a):
                continue
            if all(topo.may_write(c, d) for d in must):
                bychip.setdefault(topo.chip(c), c)
        fam.append(bychip)
    cols = []
    for ch in sorted(fam[0]):
        c0, c2 = fam[0][ch], fam[2][ch]
        c1 = [c for c in fam[1].values() if topo.mates(c0, c)][0]
        c3 = [c for c in fam[3].values() if topo.mates(c2, c)][0]
        k = [c for c in range(NCORES) if topo.host(c) == topo.host(c1) and topo.chip(c) == topo.chip(c1)
             and topo.die(c) == topo.die(c1) and c not in C and not topo.may_write(c, c0) and topo.may_write(c, c3)][0]
        cols.append([c0, c1, c2, c3, k])
    cols = cols[:W]
    where = {}
    for j, q in enumerate(cols):
        for f, c in enumerate(q):
            where[c] = (f, j)
    _CACHE["p"] = {"cols": cols, "where": where}
    return _CACHE["p"]


def _scatter_engines(topo, C, pl, r):
    sites = [pl["cols"][j][HOME[GROUP_OF[r]]] for j in range(W)]
    bits = _engines(topo, C[r], sites)
    per = len(bits) // W
    return sites, [bits[j * per:(j + 1) * per] for j in range(W)]


def _threshold(topo, C, pl, f, j, grp):
    if HOME[grp] != f:
        return len(_engines(topo, pl["cols"][j][HOME[grp]], [pl["cols"][j][f]]))
    n = sum(len(_scatter_engines(topo, C, pl, r)[1][j]) for r in GROUPS[grp])
    if grp == A_GROUP:
        n += len(_engines(topo, C[A_RANK], [pl["cols"][k][f] for k in range(W)]))
    return n


def _send(g, topo, core, d, out, in_, rsem, lsem):
    bits = _engines(topo, core, [d])
    rid, pid = topo.addr(d, core)
    g.remote_dma(out, in_, rsem, lsem, pid, rid, _join(bits))
    return len(bits)


def _rank(g, core, r, T, topo, pl):
    sem, C, v = T.sem, list(T.cores), g.vector
    sent = 0
    if r == A_RANK:
        g.sync.dma_start(T.ain[:], T.a[:]).then_inc(sem.lda, 16)
    g.sync.dma_start(T.xin[:, 0], T.x[:, 0:B]).then_inc(sem.ld0, 16)
    g.scalar.dma_start(T.xin[:, 1], T.x[:, B:2 * B]).then_inc(sem.ld1, 16)
    v.wait_ge(sem.ld0, 16)
    v.tensor_copy(T.stg[:, :, 0:w], T.xin[:, 0]).then_inc(sem.shuf, 1)
    v.wait_ge(sem.ld1, 16)
    v.tensor_copy(T.stg[:, :, w:2 * w], T.xin[:, 1]).then_inc(sem.shuf, 1)
    if r == A_RANK:
        asites = [pl["cols"][k][HOME[A_GROUP]] for k in range(W)]
        bits = _engines(topo, core, asites)
        g.wait_ge(sem.lda, 16)
        g.remote_dma_fused([RemoteDMATransfer(
            dst_ids=[_dst(topo, d, core) for d in asites], dma_engine_mask=_join(bits),
            remote_sem=sem["g%d" % A_GROUP], srcs=[T.ain[:]],
            dsts=[T.xl[:, AOFF:AOFF + P] for d in asites])], local_sem=sem.sent)
        sent += len(bits)
    sites, eng = _scatter_engines(topo, C, pl, r)
    g.wait_ge(sem.shuf, 2)
    g.remote_dma_fused([RemoteDMATransfer(
        dst_ids=[_dst(topo, sites[j], core)], dma_engine_mask=_join(eng[j]), remote_sem=sem["g%d" % GROUP_OF[r]],
        src=T.stg[:, j, :], dst=T.xl[:, XOFF[r]:XOFF[r] + PW]) for j in range(W)], local_sem=sem.sent)
    sent += sum(len(e) for e in eng)
    f = BACK_FAM if r == BACK_RANK else [k for k in range(4) if r in SERVE[k]][0]
    total = sum(len(_engines(topo, pl["cols"][j][f], [core])) for j in range(W))
    v.wait_ge(sem.sy, total)
    v.tensor_copy(T.yo[:, 0], T.yl[:, :, 0:w]).then_inc(sem.un0, 1)
    v.tensor_copy(T.yo[:, 1], T.yl[:, :, w:2 * w]).then_inc(sem.un1, 1)
    g.sync.wait_ge(sem.un0, 1)
    g.sync.dma_start(T.y[:, 0:B], T.yo[:, 0]).then_inc(sem.st, 16)
    g.scalar.wait_ge(sem.un1, 1)
    g.scalar.dma_start(T.y[:, B:2 * B], T.yo[:, 1]).then_inc(sem.st, 16)
    g.wait_ge(sem.sent, sent)
    g.wait_ge(sem.st, 32)


def _relay(g, core, j, T, topo, pl):
    sem, C = T.sem, list(T.cores)
    grp = GROUP_OF[A_RANK]
    piece = T.xl[:, GOFF[grp]:GOFF[grp] + GSIZE[grp]]
    g.wait_ge(sem["g%d" % grp], _threshold(topo, C, pl, 4, j, grp))
    n = _send(g, topo, core, pl["cols"][j][FWD[grp]], piece, piece, sem["g%d" % grp], sem.sent)
    g.wait_ge(sem.sent, n)


def _site(g, core, f, j, T, topo, pl):
    sem, C, col = T.sem, list(T.cores), pl["cols"][j]
    pe, act = g.tensor, g.scalar
    t0 = T0[f]
    nt = T0[NEXT[f]] if NEXT[f] is not None else S * (max(SERVE[f]) + 1)
    thr = {grp: _threshold(topo, C, pl, f, j, grp) for grp in NEED[f]}
    ps = [T.ps0, T.ps1]
    a_ap = T.xl[:, AOFF:AOFF + P]
    prev = [k for k in range(4) if NEXT[k] == f]
    n_in = len(_engines(topo, col[prev[0]], [core])) if prev else 0

    def x_of(t):
        o = XOFF[t // S] + (t % S) * w
        return T.xl[:, o:o + w]

    def h_of(t):
        return T.hb[:, t * w:(t + 1) * w]

    def y_of(r):
        return T.hb[:, r * PW:(r + 1) * PW]

    g.vector.memset(T.ones[:], 1.0).then_inc(sem.ms, 1)
    g.wait_ge(sem.ms, 1)
    g.affine_select(T.ident[:], T.ones[:], [[-1, P]], AluOpType.is_equal, 0.0, 0, 1).then_inc(sem.idn, 1)
    sent = 0
    for grp in NEED[f]:
        if HOME[grp] == f and FWD[grp] is not None:
            piece = T.xl[:, GOFF[grp]:GOFF[grp] + GSIZE[grp]]
            g.wait_ge(sem["g%d" % grp], thr[grp])
            sent += _send(g, topo, core, col[FWD[grp]], piece, piece, sem["g%d" % grp], sem.sent)
    if NEXT[f] is not None:
        g.wait_ge(sem["g%d" % A_GROUP], thr[A_GROUP])
        sent += _send(g, topo, core, col[NEXT[f]], a_ap, a_ap, sem.ga, sem.sent)
        g.wait_ge(sem.act, nt - t0)
        sent += _send(g, topo, core, col[NEXT[f]], h_of(nt - 1), h_of(nt - 1), sem.hh, sem.sent)
    for r in SERVE[f]:
        g.wait_ge(sem.act, S * r + S - t0)
        if r == BACK_RANK:
            sent += _send(g, topo, core, col[BACK_FAM], y_of(r), y_of(r), sem.yr, sem.sent)
        else:
            sent += _send(g, topo, core, C[r], T.yl[:, j, :], y_of(r), sem.sy, sem.sent)
    if f == BACK_FAM:
        src = col[[k for k in range(4) if BACK_RANK in SERVE[k]][0]]
        g.wait_ge(sem.yr, len(_engines(topo, src, [core])))
        sent += _send(g, topo, core, C[BACK_RANK], T.yl[:, j, :], y_of(BACK_RANK), sem.sy, sem.sent)
    g.wait_ge(sem.sent, sent)

    seen = set()

    def need(grp):
        if grp not in seen:
            seen.add(grp)
            pe.wait_ge(sem["g%d" % grp], thr[grp])

    def pre(t):
        need(GROUP_OF[t // S])
        pe.matmul(ps[t % 2][:, 0:w], T.ident[:], x_of(t), True, False)

    first = t0 if prev else t0 + 1
    pe.wait_ge(sem.idn, 1)
    pre(first)
    for t in range(first, nt):
        if t == first:
            if prev:
                pe.wait_ge(sem.ga, n_in)
            else:
                need(A_GROUP)
        if t == t0:
            pe.wait_ge(sem.hh, n_in)
        else:
            pe.wait_ge(sem.act, t - t0)
        pe.matmul(ps[t % 2][:, 0:w], a_ap, h_of(t - 1), False, True).then_inc(sem.mm, 1)
        if t + 1 < nt:
            pre(t + 1)

    if not prev:
        act.wait_ge(sem["g%d" % GROUP_OF[0]], thr[GROUP_OF[0]])
        act.activation(h_of(0), x_of(0), ActivationFunctionType.Tanh).then_inc(sem.act, 1)
    for t in range(first, nt):
        act.wait_ge(sem.mm, t - first + 1)
        act.activation(h_of(t), ps[t % 2][:, 0:w], ActivationFunctionType.Tanh).then_inc(sem.act, 1)


def rank_program(g, core, T, topo):
    pl = _plan(T, topo)
    r = T.rank_of(core)
    if r is not None:
        _rank(g, core, r, T, topo, pl)
    elif core in pl["where"]:
        f, j = pl["where"][core]
        if f == 4:
            _relay(g, core, j, T, topo, pl)
        else:
            _site(g, core, f, j, T, topo, pl)
